import numpy as np
import ml_dtypes


def mxq(x, axis, fmt="e4m3"):
    dtype, down = {"e4m3": (ml_dtypes.float8_e4m3fn, 7), "e5m2": (ml_dtypes.float8_e5m2, 14)}[fmt]
    v = np.moveaxis(np.asarray(x, np.float32).astype(ml_dtypes.bfloat16).astype(np.float64), axis, -1)
    blocks = v.reshape(v.shape[:-1] + (-1, 32))
    amax = np.abs(blocks).max(-1, keepdims=True)
    byte = np.maximum(np.where(amax > 0, np.frexp(amax)[1] - 1 + 127, 0) - down, 1)
    scale = np.exp2(byte - 127.0)
    codes = (blocks / scale).astype(np.float32).astype(dtype).astype(np.float64)
    return np.moveaxis((codes * scale).reshape(v.shape), -1, axis)


WIDE = False


def mx_kscale(k, group=512):
    if not WIDE:
        return np.ones(k)
    levels = np.array([18, -18])
    if group != 512:
        return np.exp2(np.random.permutation(np.resize(levels, k // group))).repeat(group)
    if k % 512:
        return np.exp2(np.random.permutation(np.resize(levels, k // 32))).repeat(32)
    a = np.empty((k // 512, 16))
    for p in range(k // 512):
        a[p, :8] = np.random.permutation(np.resize(levels, 8))
        for g in range(8):
            far = levels[np.abs(levels - a[p, g]) >= 10]
            a[p, g + 8] = far[np.random.randint(len(far))]
    return np.exp2(a.ravel()).repeat(32)


def f64(x):
    return np.asarray(x).astype(np.float64)


G, D, M, N = 4, 128, 128, 512


def setup_inputs():
    n = np.random.standard_normal
    s_d = mx_kscale(D, 0)
    return {
        "x": (n((G, D, N)) * s_d[:, None]).astype(np.float32),
        "w1": (n((G, D, M)) / np.sqrt(D) / s_d[:, None]).astype(np.float32),
        "w2": (n((G, D, M)) / np.sqrt(D) / s_d[:, None]).astype(np.float32),
        "dx": (n((G, D, N)) * s_d[:, None]).astype(np.float32),
        "og": (np.random.uniform(0.5, 2.0, (G, M, 1))).astype(np.float32),
        "base": (0.3 * n((G, M, N))).astype(np.float32),
    }


def reference(x, w1, w2, dx, og, base):
    w1q = mxq(f64(w1), 1, "e4m3")
    xq = mxq(f64(x), 1, "e4m3")
    z1 = w1q.transpose(0, 2, 1) @ xq
    dxq = mxq(f64(dx), 1, "e4m3")
    tz1 = w1q.transpose(0, 2, 1) @ dxq
    w2q = mxq(f64(w2), 1, "e4m3")
    z2 = w2q.transpose(0, 2, 1) @ xq
    tz2 = w2q.transpose(0, 2, 1) @ dxq
    pr = z1 * z2
    mu = np.mean(pr, axis=-1, keepdims=True)
    ms = np.sqrt(np.mean(np.square(z1), axis=-1, keepdims=True) + 0.1)
    xpr = tz1 * z2 + tz2 * z1
    xmu = np.mean(xpr, axis=-1, keepdims=True)
    xms = np.mean(tz1 * z1 * 2.0, axis=-1, keepdims=True) * 0.5 / ms
    xh = (xpr - xmu - xms * (pr - mu) / ms) / ms
    y = xh * f64(og) + f64(base)
    return y

@@ -1,0 +1,210 @@
+from contextlib import ExitStack
+
+import concourse.mybir as mybir
+
+G, D, M, N = 4, 128, 128, 512
+FLOPS = 2 * 4 * G * D * M * N
+
+F32 = mybir.dt.float32
+BF16 = mybir.dt.bfloat16
+U32 = mybir.dt.uint32
+U8 = mybir.dt.uint8
+FP8X4 = mybir.dt.float8_e4m3fn_x4
+ACT = mybir.ActivationFunctionType
+ALU = mybir.AluOpType
+
+P = 128
+PACK = 4
+ROWS = D // PACK
+HALF = N // 2
+LINE = 4
+SCALAR_COLS = 80
+EPS = 0.1
+
+
+def tile_rows_tnrowcorr_kernel(tc, x, w1, w2, dx, og, base, out):
+    nc = tc.nc
+
+    with ExitStack() as ctx:
+        sb = ctx.enter_context(tc.tile_pool(name="sb", bufs=1))
+        ps = ctx.enter_context(tc.psum_pool(name="ps", bufs=1))
+        ctx.enter_context(tc.manual_schedule())
+
+        def load(src, cols, name):
+            width = cols.stop - cols.start
+            raw = sb.tile([P, PACK, width], F32, name=name)
+            nc.sync.dma_start(out=raw[:], in_=src.rearrange("g (p j) c -> (g p) j c", j=PACK)[:, :, cols])
+            return raw
+
+        def words(width, name):
+            return sb.tile([P, width, PACK], BF16, name=name, align_bytes=64)
+
+        def interleave(copy, grouped, raw, cols):
+            copy(
+                out=grouped[:, cols, :].rearrange("p (c i) j -> p c j i", i=LINE),
+                in_=raw[:, :, cols].rearrange("p j (c i) -> p c j i", i=LINE),
+            )
+
+        def operand(width, name):
+            codes = sb.tile([P, width], U32, name=name + "_codes", align_bytes=64)
+            scales = sb.tile([P, width], U8, name=name + "_scales", align_bytes=64)
+            return codes, scales
+
+        def quantize(target, cols, grouped):
+            codes, scales = target
+            nc.vector.quantize_mx(
+                out=codes[:, cols].bitcast(FP8X4),
+                scales=scales[:, cols],
+                in_=grouped[:].rearrange("p c j -> p (c j)"),
+            )
+
+        def product(bank, weights, inputs, g):
+            rows = slice(ROWS * g, ROWS * (g + 1))
+            nc.tensor.matmul_mx(
+                out=bank[:],
+                lhsT=weights[0][rows, :].bitcast(FP8X4),
+                lhsT_scale=weights[1][rows, :],
+                rhs=inputs[0][rows, :].bitcast(FP8X4),
+                rhs_scale=inputs[1][rows, :],
+                start=True,
+                stop=True,
+            )
+
+        def columns(name):
+            return [sb.tile([P, 1], F32, name="%s%d" % (name, g)) for g in range(G)]
+
+        def rows_of(name):
+            return [sb.tile([P, N], F32, name="%s%d" % (name, g)) for g in range(G)]
+
+        halves = [slice(0, HALF), slice(HALF, N)]
+        all_m = slice(0, M)
+        all_half = slice(0, HALF)
+
+        w1_raw = load(w1, all_m, "w1_raw")
+        x_raw = [load(x, halves[h], "x_raw%d" % h) for h in range(2)]
+        w2_raw = load(w2, all_m, "w2_raw")
+        dx_raw = [load(dx, halves[h], "dx_raw%d" % h) for h in range(2)]
+        base_sb = rows_of("base")
+        for g in range(G):
+            nc.sync.dma_start(out=base_sb[g][:], in_=base[g])
+
+        og_rows = sb.tile([P, P], F32, name="og_rows", align_bytes=64)
+        og_cols = sb.tile([P, P], F32, name="og_cols", align_bytes=64)
+        eps = sb.tile([P, 1], F32, name="eps")
+        nc.vector.memset(og_rows[:], 0.0)
+        nc.vector.memset(eps[:], 100.0)
+        nc.scalar.dma_start(
+            out=og_rows[0:P:32, :].rearrange("q (g i) -> q g i", g=G),
+            in_=og.rearrange("g (q i) o -> q g (i o)", i=32),
+        )
+        nc.scalar.activation(out=eps[:], in_=eps[:], func=ACT.Abs_reciprocal_sqrt)
+        gain = [og_cols[:, 32 * g : 32 * g + 1] for g in range(G)]
+
+        w1_q, w2_q = operand(M, "w1"), operand(M, "w2")
+        x_q, dx_q = operand(N, "x"), operand(N, "dx")
+        w1_words, w2_words = words(M, "w1_words"), words(M, "w2_words")
+        x_words = [words(HALF, "x_words%d" % h) for h in range(2)]
+        dx_words = [words(HALF, "dx_words%d" % h) for h in range(2)]
+
+        interleave(nc.vector.tensor_copy, w1_words, w1_raw, all_m)
+        nc.vector.transpose(out=og_cols[:], in_=og_rows[:])
+        quantize(w1_q, all_m, w1_words)
+        interleave(nc.vector.tensor_copy, x_words[0], x_raw[0], all_half)
+        quantize(x_q, halves[0], x_words[0])
+        interleave(nc.scalar.copy, x_words[1], x_raw[1], slice(0, SCALAR_COLS))
+        interleave(nc.vector.tensor_copy, x_words[1], x_raw[1], slice(SCALAR_COLS, HALF))
+        quantize(x_q, halves[1], x_words[1])
+
+        bank_a = [ps.tile([P, N], F32, name="bank_a%d" % g) for g in range(G)]
+        bank_b = [ps.tile([P, N], F32, name="bank_b%d" % g) for g in range(G)]
+        for g in range(G):
+            product(bank_a[g], w1_q, x_q, g)
+
+        interleave(nc.vector.tensor_copy, w2_words, w2_raw, all_m)
+        quantize(w2_q, all_m, w2_words)
+        for h in range(2):
+            interleave(nc.vector.tensor_copy, dx_words[h], dx_raw[h], all_half)
+            quantize(dx_q, halves[h], dx_words[h])
+
+        sum_sq, inv_ms, gain_inv = columns("sum_sq"), columns("inv_ms"), columns("gain_inv")
+        neg_c, sum_p, sum_q = columns("neg_c"), columns("sum_p"), columns("sum_q")
+        neg_mean_q, neg_mean = columns("neg_mean_q"), columns("neg_mean")
+        z1n, u, p_term, q_term = rows_of("z1n"), rows_of("u"), rows_of("p_term"), rows_of("q_term")
+        result = rows_of("result")
+
+        def normalise(g):
+            nc.scalar.activation(out=z1n[g][:], in_=bank_a[g][:], func=ACT.Square, accum_out=sum_sq[g][:])
+            nc.scalar.activation(
+                out=inv_ms[g][:], in_=sum_sq[g][:], func=ACT.Abs_reciprocal_sqrt, scale=1.0 / N, bias=eps[:]
+            )
+            nc.scalar.activation(out=z1n[g][:], in_=bank_a[g][:], func=ACT.Copy, scale=inv_ms[g][:])
+            nc.scalar.activation(out=gain_inv[g][:], in_=inv_ms[g][:], func=ACT.Copy, scale=gain[g])
+
+        def make_q(g):
+            nc.vector.scalar_tensor_tensor(
+                out=q_term[g][:], in0=bank_b[g][:], scalar=gain[g], in1=z1n[g][:],
+                op0=ALU.mult, op1=ALU.mult, accum_out=sum_q[g][:],
+            )
+            product(bank_b[g], w2_q, x_q, g)
+            nc.gpsimd.tensor_tensor(out=q_term[g][:], in0=q_term[g][:], in1=base_sb[g][:], op=ALU.add)
+
+        def make_c(g):
+            nc.vector.scalar_tensor_tensor(
+                out=u[g][:], in0=bank_a[g][:], scalar=-1.0 / N, in1=z1n[g][:],
+                op0=ALU.mult, op1=ALU.mult, accum_out=neg_c[g][:],
+            )
+
+        def make_u(g):
+            nc.vector.scalar_tensor_tensor(
+                out=u[g][:], in0=z1n[g][:], scalar=neg_c[g][:], in1=bank_a[g][:], op0=ALU.mult, op1=ALU.add
+            )
+
+        def make_p(g):
+            nc.vector.scalar_tensor_tensor(
+                out=p_term[g][:], in0=bank_b[g][:], scalar=gain_inv[g][:], in1=u[g][:],
+                op0=ALU.mult, op1=ALU.mult, accum_out=sum_p[g][:],
+            )
+
+        def finish(g):
+            nc.gpsimd.tensor_tensor(out=p_term[g][:], in0=p_term[g][:], in1=q_term[g][:], op=ALU.add)
+            nc.scalar.activation(out=neg_mean_q[g][:], in_=sum_q[g][:], func=ACT.Copy, scale=-1.0 / N)
+            nc.scalar.activation(
+                out=neg_mean[g][:], in_=sum_p[g][:], func=ACT.Identity, scale=-1.0 / N, bias=neg_mean_q[g][:]
+            )
+            nc.scalar.activation(out=result[g][:], in_=p_term[g][:], func=ACT.Identity, bias=neg_mean[g][:])
+            nc.sync.dma_start(out=out[g], in_=result[g][:])
+
+        def finish_last(g):
+            nc.vector.tensor_scalar(
+                out=neg_mean[g][:], in0=sum_p[g][:], scalar1=sum_q[g][:], scalar2=-1.0 / N, op0=ALU.add, op1=ALU.mult
+            )
+            for cols in halves:
+                nc.vector.scalar_tensor_tensor(
+                    out=result[g][:, cols], in0=p_term[g][:, cols], scalar=neg_mean[g][:], in1=q_term[g][:, cols],
+                    op0=ALU.add, op1=ALU.add,
+                )
+                nc.sync.dma_start(out=out[g][:, cols], in_=result[g][:, cols])
+
+        normalise(0)
+        product(bank_b[0], w2_q, dx_q, 0)
+        product(bank_a[0], w1_q, dx_q, 0)
+        for g in range(1, G):
+            product(bank_b[g], w2_q, dx_q, g)
+        normalise(1)
+        product(bank_a[1], w1_q, dx_q, 1)
+        make_q(0)
+        for g in range(G):
+            if g + 2 < G:
+                normalise(g + 2)
+                product(bank_a[g + 2], w1_q, dx_q, g + 2)
+            make_c(g)
+            if g == 0:
+                make_q(1)
+            else:
+                make_p(g - 1)
+                finish(g - 1)
+            make_u(g)
+            if 0 < g < G - 1:
+                make_q(g + 1)
+        make_p(G - 1)
+        finish_last(G - 1)

@@ -18,7 +18,7 @@ PACK = 4
 ROWS = D // PACK
 HALF = N // 2
 LINE = 4
-SCALAR_COLS = 80
+SCALAR_COLS = 160
 EPS = 0.1
 
 
@@ -50,12 +50,13 @@ def tile_rows_tnrowcorr_kernel(tc, x, w1, w2, dx, og, base, out):
             scales = sb.tile([P, width], U8, name=name + "_scales", align_bytes=64)
             return codes, scales
 
-        def quantize(target, cols, grouped):
+        def quantize(target, grouped, cols, first=0):
             codes, scales = target
+            to = slice(first + cols.start, first + cols.stop)
             nc.vector.quantize_mx(
-                out=codes[:, cols].bitcast(FP8X4),
-                scales=scales[:, cols],
-                in_=grouped[:].rearrange("p c j -> p (c j)"),
+                out=codes[:, to].bitcast(FP8X4),
+                scales=scales[:, to],
+                in_=grouped[:, cols, :].rearrange("p c j -> p (c j)"),
             )
 
         def product(bank, weights, inputs, g):
@@ -78,12 +79,14 @@ def tile_rows_tnrowcorr_kernel(tc, x, w1, w2, dx, og, base, out):
 
         halves = [slice(0, HALF), slice(HALF, N)]
         all_m = slice(0, M)
+        all_n = slice(0, N)
         all_half = slice(0, HALF)
+        quarters = [slice(0, HALF // 2), slice(HALF // 2, HALF)]
 
+        x_raw = load(x, all_n, "x_raw")
         w1_raw = load(w1, all_m, "w1_raw")
-        x_raw = [load(x, halves[h], "x_raw%d" % h) for h in range(2)]
-        w2_raw = load(w2, all_m, "w2_raw")
         dx_raw = [load(dx, halves[h], "dx_raw%d" % h) for h in range(2)]
+        w2_raw = load(w2, all_m, "w2_raw")
         base_sb = rows_of("base")
         for g in range(G):
             nc.sync.dma_start(out=base_sb[g][:], in_=base[g])
@@ -103,28 +106,30 @@ def tile_rows_tnrowcorr_kernel(tc, x, w1, w2, dx, og, base, out):
         w1_q, w2_q = operand(M, "w1"), operand(M, "w2")
         x_q, dx_q = operand(N, "x"), operand(N, "dx")
         w1_words, w2_words = words(M, "w1_words"), words(M, "w2_words")
-        x_words = [words(HALF, "x_words%d" % h) for h in range(2)]
+        x_words = words(N, "x_words")
         dx_words = [words(HALF, "dx_words%d" % h) for h in range(2)]
 
-        interleave(nc.vector.tensor_copy, w1_words, w1_raw, all_m)
-        nc.vector.transpose(out=og_cols[:], in_=og_rows[:])
-        quantize(w1_q, all_m, w1_words)
-        interleave(nc.vector.tensor_copy, x_words[0], x_raw[0], all_half)
-        quantize(x_q, halves[0], x_words[0])
-        interleave(nc.scalar.copy, x_words[1], x_raw[1], slice(0, SCALAR_COLS))
-        interleave(nc.vector.tensor_copy, x_words[1], x_raw[1], slice(SCALAR_COLS, HALF))
-        quantize(x_q, halves[1], x_words[1])
+        interleave(nc.scalar.copy, x_words, x_raw, slice(0, SCALAR_COLS))
+        interleave(nc.vector.tensor_copy, x_words, x_raw, slice(SCALAR_COLS, HALF))
+        interleave(nc.vector.tensor_copy, x_words, x_raw, halves[1])
+        interleave(nc.scalar.copy, w1_words, w1_raw, all_m)
+        for cols in halves:
+            quantize(x_q, x_words, cols)
+        quantize(w1_q, w1_words, all_m)
 
         bank_a = [ps.tile([P, N], F32, name="bank_a%d" % g) for g in range(G)]
         bank_b = [ps.tile([P, N], F32, name="bank_b%d" % g) for g in range(G)]
         for g in range(G):
             product(bank_a[g], w1_q, x_q, g)
 
-        interleave(nc.vector.tensor_copy, w2_words, w2_raw, all_m)
-        quantize(w2_q, all_m, w2_words)
         for h in range(2):
-            interleave(nc.vector.tensor_copy, dx_words[h], dx_raw[h], all_half)
-            quantize(dx_q, halves[h], dx_words[h])
+            for cols in quarters:
+                interleave(nc.vector.tensor_copy, dx_words[h], dx_raw[h], cols)
+            for cols in quarters:
+                quantize(dx_q, dx_words[h], cols, halves[h].start)
+        interleave(nc.vector.tensor_copy, w2_words, w2_raw, all_m)
+        nc.vector.transpose(out=og_cols[:], in_=og_rows[:])
+        quantize(w2_q, w2_words, all_m)
 
         sum_sq, inv_ms, gain_inv = columns("sum_sq"), columns("inv_ms"), columns("gain_inv")
         neg_c, sum_p, sum_q = columns("neg_c"), columns("sum_p"), columns("sum_q")
@@ -132,79 +137,89 @@ def tile_rows_tnrowcorr_kernel(tc, x, w1, w2, dx, og, base, out):
         z1n, u, p_term, q_term = rows_of("z1n"), rows_of("u"), rows_of("p_term"), rows_of("q_term")
         result = rows_of("result")
 
+        def make_gain_inv(g):
+            nc.scalar.activation(out=gain_inv[g][:], in_=inv_ms[g][:], func=ACT.Copy, scale=gain[g])
+
         def normalise(g):
             nc.scalar.activation(out=z1n[g][:], in_=bank_a[g][:], func=ACT.Square, accum_out=sum_sq[g][:])
+            if g > 0:
+                make_gain_inv(g - 1)
             nc.scalar.activation(
                 out=inv_ms[g][:], in_=sum_sq[g][:], func=ACT.Abs_reciprocal_sqrt, scale=1.0 / N, bias=eps[:]
             )
             nc.scalar.activation(out=z1n[g][:], in_=bank_a[g][:], func=ACT.Copy, scale=inv_ms[g][:])
-            nc.scalar.activation(out=gain_inv[g][:], in_=inv_ms[g][:], func=ACT.Copy, scale=gain[g])
+            if g == G - 1:
+                make_gain_inv(g)
 
         def make_q(g):
             nc.vector.scalar_tensor_tensor(
-                out=q_term[g][:], in0=bank_b[g][:], scalar=gain[g], in1=z1n[g][:],
+                out=q_term[g][:], in0=bank_a[g][:], scalar=gain[g], in1=z1n[g][:],
                 op0=ALU.mult, op1=ALU.mult, accum_out=sum_q[g][:],
             )
-            product(bank_b[g], w2_q, x_q, g)
+            product(bank_a[g], w2_q, x_q, g)
             nc.gpsimd.tensor_tensor(out=q_term[g][:], in0=q_term[g][:], in1=base_sb[g][:], op=ALU.add)
 
         def make_c(g):
             nc.vector.scalar_tensor_tensor(
-                out=u[g][:], in0=bank_a[g][:], scalar=-1.0 / N, in1=z1n[g][:],
+                out=u[g][:], in0=bank_b[g][:], scalar=-1.0 / N, in1=z1n[g][:],
                 op0=ALU.mult, op1=ALU.mult, accum_out=neg_c[g][:],
             )
 
         def make_u(g):
             nc.vector.scalar_tensor_tensor(
-                out=u[g][:], in0=z1n[g][:], scalar=neg_c[g][:], in1=bank_a[g][:], op0=ALU.mult, op1=ALU.add
+                out=u[g][:], in0=z1n[g][:], scalar=neg_c[g][:], in1=bank_b[g][:], op0=ALU.mult, op1=ALU.add
             )
 
         def make_p(g):
             nc.vector.scalar_tensor_tensor(
-                out=p_term[g][:], in0=bank_b[g][:], scalar=gain_inv[g][:], in1=u[g][:],
+                out=p_term[g][:], in0=bank_a[g][:], scalar=gain_inv[g][:], in1=u[g][:],
                 op0=ALU.mult, op1=ALU.mult, accum_out=sum_p[g][:],
             )
 
-        def finish(g):
-            nc.gpsimd.tensor_tensor(out=p_term[g][:], in0=p_term[g][:], in1=q_term[g][:], op=ALU.add)
+        def make_mean(g):
             nc.scalar.activation(out=neg_mean_q[g][:], in_=sum_q[g][:], func=ACT.Copy, scale=-1.0 / N)
             nc.scalar.activation(
                 out=neg_mean[g][:], in_=sum_p[g][:], func=ACT.Identity, scale=-1.0 / N, bias=neg_mean_q[g][:]
             )
+
+        def finish_off_vector(g):
+            nc.gpsimd.tensor_tensor(out=p_term[g][:], in0=p_term[g][:], in1=q_term[g][:], op=ALU.add)
             nc.scalar.activation(out=result[g][:], in_=p_term[g][:], func=ACT.Identity, bias=neg_mean[g][:])
-            nc.sync.dma_start(out=out[g], in_=result[g][:])
+            nc.scalar.dma_start(out=out[g], in_=result[g][:])
 
-        def finish_last(g):
-            nc.vector.tensor_scalar(
-                out=neg_mean[g][:], in0=sum_p[g][:], scalar1=sum_q[g][:], scalar2=-1.0 / N, op0=ALU.add, op1=ALU.mult
+        def finish_on_vector(g, cols):
+            nc.vector.scalar_tensor_tensor(
+                out=result[g][:, cols], in0=p_term[g][:, cols], scalar=neg_mean[g][:], in1=q_term[g][:, cols],
+                op0=ALU.add, op1=ALU.add,
             )
-            for cols in halves:
-                nc.vector.scalar_tensor_tensor(
-                    out=result[g][:, cols], in0=p_term[g][:, cols], scalar=neg_mean[g][:], in1=q_term[g][:, cols],
-                    op0=ALU.add, op1=ALU.add,
-                )
-                nc.sync.dma_start(out=out[g][:, cols], in_=result[g][:, cols])
+            nc.sync.dma_start(out=out[g][:, cols], in_=result[g][:, cols])
 
-        normalise(0)
-        product(bank_b[0], w2_q, dx_q, 0)
-        product(bank_a[0], w1_q, dx_q, 0)
-        for g in range(1, G):
-            product(bank_b[g], w2_q, dx_q, g)
-        normalise(1)
-        product(bank_a[1], w1_q, dx_q, 1)
-        make_q(0)
+        def tangents(g):
+            product(bank_b[g], w1_q, dx_q, g)
+            product(bank_a[g], w2_q, dx_q, g)
+
+        for g in range(2):
+            normalise(g)
+            tangents(g)
         for g in range(G):
             if g + 2 < G:
                 normalise(g + 2)
-                product(bank_a[g + 2], w1_q, dx_q, g + 2)
             make_c(g)
             if g == 0:
-                make_q(1)
+                make_q(0)
             else:
                 make_p(g - 1)
-                finish(g - 1)
+                make_mean(g - 1)
+                if g - 1 < G - 2:
+                    finish_off_vector(g - 1)
             make_u(g)
-            if 0 < g < G - 1:
+            if g + 1 < G:
                 make_q(g + 1)
+            if g + 2 < G:
+                tangents(g + 2)
+        finish_on_vector(G - 2, halves[0])
         make_p(G - 1)
-        finish_last(G - 1)
+        make_mean(G - 1)
+        finish_on_vector(G - 2, halves[1])
+        for cols in halves:
+            finish_on_vector(G - 1, cols)

@@ -18,7 +18,7 @@ PACK = 4
 ROWS = D // PACK
 HALF = N // 2
 LINE = 4
-SCALAR_COLS = 160
+SCALAR_COLS = 96
 EPS = 0.1
 
 
@@ -79,11 +79,9 @@ def tile_rows_tnrowcorr_kernel(tc, x, w1, w2, dx, og, base, out):
 
         halves = [slice(0, HALF), slice(HALF, N)]
         all_m = slice(0, M)
-        all_n = slice(0, N)
-        all_half = slice(0, HALF)
         quarters = [slice(0, HALF // 2), slice(HALF // 2, HALF)]
 
-        x_raw = load(x, all_n, "x_raw")
+        x_raw = [load(x, halves[h], "x_raw%d" % h) for h in range(2)]
         w1_raw = load(w1, all_m, "w1_raw")
         dx_raw = [load(dx, halves[h], "dx_raw%d" % h) for h in range(2)]
         w2_raw = load(w2, all_m, "w2_raw")
@@ -106,15 +104,18 @@ def tile_rows_tnrowcorr_kernel(tc, x, w1, w2, dx, og, base, out):
         w1_q, w2_q = operand(M, "w1"), operand(M, "w2")
         x_q, dx_q = operand(N, "x"), operand(N, "dx")
         w1_words, w2_words = words(M, "w1_words"), words(M, "w2_words")
-        x_words = words(N, "x_words")
+        x_words = [words(HALF, "x_words%d" % h) for h in range(2)]
         dx_words = [words(HALF, "dx_words%d" % h) for h in range(2)]
 
-        interleave(nc.scalar.copy, x_words, x_raw, slice(0, SCALAR_COLS))
-        interleave(nc.vector.tensor_copy, x_words, x_raw, slice(SCALAR_COLS, HALF))
-        interleave(nc.vector.tensor_copy, x_words, x_raw, halves[1])
-        interleave(nc.scalar.copy, w1_words, w1_raw, all_m)
-        for cols in halves:
-            quantize(x_q, x_words, cols)
+        for cols in quarters:
+            interleave(nc.vector.tensor_copy, x_words[0], x_raw[0], cols)
+        for cols in quarters:
+            quantize(x_q, x_words[0], cols)
+        interleave(nc.scalar.copy, x_words[1], x_raw[1], slice(0, SCALAR_COLS))
+        interleave(nc.vector.tensor_copy, x_words[1], x_raw[1], slice(SCALAR_COLS, HALF))
+        interleave(nc.scalar.copy, w1_words, w1_raw, slice(0, M // 2))
+        interleave(nc.vector.tensor_copy, w1_words, w1_raw, slice(M // 2, M))
+        quantize(x_q, x_words[1], slice(0, HALF), HALF)
         quantize(w1_q, w1_words, all_m)
 
         bank_a = [ps.tile([P, N], F32, name="bank_a%d" % g) for g in range(G)]
@@ -122,17 +123,8 @@ def tile_rows_tnrowcorr_kernel(tc, x, w1, w2, dx, og, base, out):
         for g in range(G):
             product(bank_a[g], w1_q, x_q, g)
 
-        for h in range(2):
-            for cols in quarters:
-                interleave(nc.vector.tensor_copy, dx_words[h], dx_raw[h], cols)
-            for cols in quarters:
-                quantize(dx_q, dx_words[h], cols, halves[h].start)
-        interleave(nc.vector.tensor_copy, w2_words, w2_raw, all_m)
-        nc.vector.transpose(out=og_cols[:], in_=og_rows[:])
-        quantize(w2_q, w2_words, all_m)
-
         sum_sq, inv_ms, gain_inv = columns("sum_sq"), columns("inv_ms"), columns("gain_inv")
-        neg_c, sum_p, sum_q = columns("neg_c"), columns("sum_p"), columns("sum_q")
+        neg_c, sum_p = columns("neg_c"), columns("sum_p")
         neg_mean_q, neg_mean = columns("neg_mean_q"), columns("neg_mean")
         z1n, u, p_term, q_term = rows_of("z1n"), rows_of("u"), rows_of("p_term"), rows_of("q_term")
         result = rows_of("result")
@@ -154,10 +146,10 @@ def tile_rows_tnrowcorr_kernel(tc, x, w1, w2, dx, og, base, out):
         def make_q(g):
             nc.vector.scalar_tensor_tensor(
                 out=q_term[g][:], in0=bank_a[g][:], scalar=gain[g], in1=z1n[g][:],
-                op0=ALU.mult, op1=ALU.mult, accum_out=sum_q[g][:],
+                op0=ALU.mult, op1=ALU.mult,
             )
             product(bank_a[g], w2_q, x_q, g)
-            nc.gpsimd.tensor_tensor(out=q_term[g][:], in0=q_term[g][:], in1=base_sb[g][:], op=ALU.add)
+            nc.gpsimd.tensor_tensor(out=base_sb[g][:], in0=q_term[g][:], in1=base_sb[g][:], op=ALU.add)
 
         def make_c(g):
             nc.vector.scalar_tensor_tensor(
@@ -176,20 +168,26 @@ def tile_rows_tnrowcorr_kernel(tc, x, w1, w2, dx, og, base, out):
                 op0=ALU.mult, op1=ALU.mult, accum_out=sum_p[g][:],
             )
 
+        def mean_of_q(g):
+            nc.scalar.activation(
+                out=result[g][:], in_=q_term[g][:], func=ACT.Copy, scale=-1.0 / N, accum_out=neg_mean_q[g][:]
+            )
+
         def make_mean(g):
-            nc.scalar.activation(out=neg_mean_q[g][:], in_=sum_q[g][:], func=ACT.Copy, scale=-1.0 / N)
             nc.scalar.activation(
                 out=neg_mean[g][:], in_=sum_p[g][:], func=ACT.Identity, scale=-1.0 / N, bias=neg_mean_q[g][:]
             )
 
-        def finish_off_vector(g):
-            nc.gpsimd.tensor_tensor(out=p_term[g][:], in0=p_term[g][:], in1=q_term[g][:], op=ALU.add)
-            nc.scalar.activation(out=result[g][:], in_=p_term[g][:], func=ACT.Identity, bias=neg_mean[g][:])
+        def add_p(g):
+            nc.gpsimd.tensor_tensor(out=base_sb[g][:], in0=p_term[g][:], in1=base_sb[g][:], op=ALU.add)
+
+        def centre_and_store(g):
+            nc.scalar.activation(out=result[g][:], in_=base_sb[g][:], func=ACT.Identity, bias=neg_mean[g][:])
             nc.scalar.dma_start(out=out[g], in_=result[g][:])
 
         def finish_on_vector(g, cols):
             nc.vector.scalar_tensor_tensor(
-                out=result[g][:, cols], in0=p_term[g][:, cols], scalar=neg_mean[g][:], in1=q_term[g][:, cols],
+                out=result[g][:, cols], in0=p_term[g][:, cols], scalar=neg_mean[g][:], in1=base_sb[g][:, cols],
                 op0=ALU.add, op1=ALU.add,
             )
             nc.sync.dma_start(out=out[g][:, cols], in_=result[g][:, cols])
@@ -198,28 +196,35 @@ def tile_rows_tnrowcorr_kernel(tc, x, w1, w2, dx, og, base, out):
             product(bank_b[g], w1_q, dx_q, g)
             product(bank_a[g], w2_q, dx_q, g)
 
+        for h in range(2):
+            for cols in quarters:
+                interleave(nc.vector.tensor_copy, dx_words[h], dx_raw[h], cols)
+            for cols in quarters:
+                quantize(dx_q, dx_words[h], cols, halves[h].start)
+        interleave(nc.vector.tensor_copy, w2_words, w2_raw, all_m)
+        nc.vector.transpose(out=og_cols[:], in_=og_rows[:])
+        quantize(w2_q, w2_words, all_m)
+
         for g in range(2):
             normalise(g)
             tangents(g)
         for g in range(G):
+            make_c(g)
+            make_q(g)
             if g + 2 < G:
                 normalise(g + 2)
-            make_c(g)
-            if g == 0:
-                make_q(0)
-            else:
+                tangents(g + 2)
+            mean_of_q(g)
+            if g >= 2:
+                centre_and_store(g - 2)
+            make_u(g)
+            if g > 0:
                 make_p(g - 1)
                 make_mean(g - 1)
                 if g - 1 < G - 2:
-                    finish_off_vector(g - 1)
-            make_u(g)
-            if g + 1 < G:
-                make_q(g + 1)
-            if g + 2 < G:
-                tangents(g + 2)
-        finish_on_vector(G - 2, halves[0])
+                    add_p(g - 1)
         make_p(G - 1)
         make_mean(G - 1)
-        finish_on_vector(G - 2, halves[1])
+        finish_on_vector(G - 2, slice(0, N))
         for cols in halves:
             finish_on_vector(G - 1, cols)

@@ -18,7 +18,7 @@ PACK = 4
 ROWS = D // PACK
 HALF = N // 2
 LINE = 4
-SCALAR_COLS = 96
+SCALAR_COLS_X = 160
 EPS = 0.1
 
 
@@ -81,7 +81,7 @@ def tile_rows_tnrowcorr_kernel(tc, x, w1, w2, dx, og, base, out):
         all_m = slice(0, M)
         quarters = [slice(0, HALF // 2), slice(HALF // 2, HALF)]
 
-        x_raw = [load(x, halves[h], "x_raw%d" % h) for h in range(2)]
+        x_raw = load(x, slice(0, N), "x_raw")
         w1_raw = load(w1, all_m, "w1_raw")
         dx_raw = [load(dx, halves[h], "dx_raw%d" % h) for h in range(2)]
         w2_raw = load(w2, all_m, "w2_raw")
@@ -104,23 +104,20 @@ def tile_rows_tnrowcorr_kernel(tc, x, w1, w2, dx, og, base, out):
         w1_q, w2_q = operand(M, "w1"), operand(M, "w2")
         x_q, dx_q = operand(N, "x"), operand(N, "dx")
         w1_words, w2_words = words(M, "w1_words"), words(M, "w2_words")
-        x_words = [words(HALF, "x_words%d" % h) for h in range(2)]
+        x_words = words(N, "x_words")
         dx_words = [words(HALF, "dx_words%d" % h) for h in range(2)]
 
-        for cols in quarters:
-            interleave(nc.vector.tensor_copy, x_words[0], x_raw[0], cols)
-        for cols in quarters:
-            quantize(x_q, x_words[0], cols)
-        interleave(nc.scalar.copy, x_words[1], x_raw[1], slice(0, SCALAR_COLS))
-        interleave(nc.vector.tensor_copy, x_words[1], x_raw[1], slice(SCALAR_COLS, HALF))
-        interleave(nc.scalar.copy, w1_words, w1_raw, slice(0, M // 2))
-        interleave(nc.vector.tensor_copy, w1_words, w1_raw, slice(M // 2, M))
-        quantize(x_q, x_words[1], slice(0, HALF), HALF)
+        interleave(nc.scalar.copy, x_words, x_raw, slice(0, SCALAR_COLS_X))
+        interleave(nc.vector.tensor_copy, x_words, x_raw, halves[1])
+        interleave(nc.vector.tensor_copy, x_words, x_raw, slice(SCALAR_COLS_X, HALF))
+        interleave(nc.scalar.copy, w1_words, w1_raw, all_m)
+        for cols in reversed(halves):
+            quantize(x_q, x_words, cols)
         quantize(w1_q, w1_words, all_m)
 
         bank_a = [ps.tile([P, N], F32, name="bank_a%d" % g) for g in range(G)]
         bank_b = [ps.tile([P, N], F32, name="bank_b%d" % g) for g in range(G)]
-        for g in range(G):
+        for g in range(G - 1):
             product(bank_a[g], w1_q, x_q, g)
 
         sum_sq, inv_ms, gain_inv = columns("sum_sq"), columns("inv_ms"), columns("gain_inv")
@@ -196,18 +193,22 @@ def tile_rows_tnrowcorr_kernel(tc, x, w1, w2, dx, og, base, out):
             product(bank_b[g], w1_q, dx_q, g)
             product(bank_a[g], w2_q, dx_q, g)
 
-        for h in range(2):
-            for cols in quarters:
-                interleave(nc.vector.tensor_copy, dx_words[h], dx_raw[h], cols)
-            for cols in quarters:
-                quantize(dx_q, dx_words[h], cols, halves[h].start)
+        interleave(nc.scalar.copy, dx_words[0], dx_raw[0], quarters[0])
+        interleave(nc.vector.tensor_copy, dx_words[0], dx_raw[0], quarters[1])
+        quantize(dx_q, dx_words[0], slice(0, HALF))
+        for cols in quarters:
+            interleave(nc.vector.tensor_copy, dx_words[1], dx_raw[1], cols)
+        for cols in quarters:
+            quantize(dx_q, dx_words[1], cols, HALF)
         interleave(nc.vector.tensor_copy, w2_words, w2_raw, all_m)
         nc.vector.transpose(out=og_cols[:], in_=og_rows[:])
         quantize(w2_q, w2_words, all_m)
 
-        for g in range(2):
-            normalise(g)
-            tangents(g)
+        normalise(0)
+        tangents(0)
+        product(bank_a[G - 1], w1_q, x_q, G - 1)
+        normalise(1)
+        tangents(1)
         for g in range(G):
             make_c(g)
             make_q(g)
@@ -225,6 +226,6 @@ def tile_rows_tnrowcorr_kernel(tc, x, w1, w2, dx, og, base, out):
                     add_p(g - 1)
         make_p(G - 1)
         make_mean(G - 1)
-        finish_on_vector(G - 2, slice(0, N))
-        for cols in halves:
-            finish_on_vector(G - 1, cols)
+        for g in range(G - 2, G):
+            for cols in halves:
+                finish_on_vector(g, cols)

from contextlib import ExitStack

import concourse.mybir as mybir

G, D, M, N = 4, 128, 128, 512
FLOPS = 2 * 4 * G * D * M * N

F32 = mybir.dt.float32
BF16 = mybir.dt.bfloat16
U32 = mybir.dt.uint32
U8 = mybir.dt.uint8
FP8X4 = mybir.dt.float8_e4m3fn_x4
ACT = mybir.ActivationFunctionType
ALU = mybir.AluOpType

P = 128
PACK = 4
ROWS = D // PACK
HALF = N // 2
LINE = 4
SCALAR_COLS_X = 160
EPS = 0.1


def tile_rows_tnrowcorr_kernel(tc, x, w1, w2, dx, og, base, out):
    nc = tc.nc

    with ExitStack() as ctx:
        sb = ctx.enter_context(tc.tile_pool(name="sb", bufs=1))
        ps = ctx.enter_context(tc.psum_pool(name="ps", bufs=1))
        ctx.enter_context(tc.manual_schedule())

        def load(src, cols, name):
            width = cols.stop - cols.start
            raw = sb.tile([P, PACK, width], F32, name=name)
            nc.sync.dma_start(out=raw[:], in_=src.rearrange("g (p j) c -> (g p) j c", j=PACK)[:, :, cols])
            return raw

        def words(width, name):
            return sb.tile([P, width, PACK], BF16, name=name, align_bytes=64)

        def interleave(copy, grouped, raw, cols):
            copy(
                out=grouped[:, cols, :].rearrange("p (c i) j -> p c j i", i=LINE),
                in_=raw[:, :, cols].rearrange("p j (c i) -> p c j i", i=LINE),
            )

        def operand(width, name):
            codes = sb.tile([P, width], U32, name=name + "_codes", align_bytes=64)
            scales = sb.tile([P, width], U8, name=name + "_scales", align_bytes=64)
            return codes, scales

        def quantize(target, grouped, cols, first=0):
            codes, scales = target
            to = slice(first + cols.start, first + cols.stop)
            nc.vector.quantize_mx(
                out=codes[:, to].bitcast(FP8X4),
                scales=scales[:, to],
                in_=grouped[:, cols, :].rearrange("p c j -> p (c j)"),
            )

        def product(bank, weights, inputs, g):
            rows = slice(ROWS * g, ROWS * (g + 1))
            nc.tensor.matmul_mx(
                out=bank[:],
                lhsT=weights[0][rows, :].bitcast(FP8X4),
                lhsT_scale=weights[1][rows, :],
                rhs=inputs[0][rows, :].bitcast(FP8X4),
                rhs_scale=inputs[1][rows, :],
                start=True,
                stop=True,
            )

        def columns(name):
            return [sb.tile([P, 1], F32, name="%s%d" % (name, g)) for g in range(G)]

        def rows_of(name):
            return [sb.tile([P, N], F32, name="%s%d" % (name, g)) for g in range(G)]

        halves = [slice(0, HALF), slice(HALF, N)]
        all_m = slice(0, M)
        quarters = [slice(0, HALF // 2), slice(HALF // 2, HALF)]

        x_raw = load(x, slice(0, N), "x_raw")
        w1_raw = load(w1, all_m, "w1_raw")
        dx_raw = [load(dx, halves[h], "dx_raw%d" % h) for h in range(2)]
        w2_raw = load(w2, all_m, "w2_raw")
        base_sb = rows_of("base")
        for g in range(G):
            nc.sync.dma_start(out=base_sb[g][:], in_=base[g])

        og_rows = sb.tile([P, P], F32, name="og_rows", align_bytes=64)
        og_cols = sb.tile([P, P], F32, name="og_cols", align_bytes=64)
        eps = sb.tile([P, 1], F32, name="eps")
        nc.vector.memset(og_rows[:], 0.0)
        nc.vector.memset(eps[:], 100.0)
        nc.scalar.dma_start(
            out=og_rows[0:P:32, :].rearrange("q (g i) -> q g i", g=G),
            in_=og.rearrange("g (q i) o -> q g (i o)", i=32),
        )
        nc.scalar.activation(out=eps[:], in_=eps[:], func=ACT.Abs_reciprocal_sqrt)
        gain = [og_cols[:, 32 * g : 32 * g + 1] for g in range(G)]

        w1_q, w2_q = operand(M, "w1"), operand(M, "w2")
        x_q, dx_q = operand(N, "x"), operand(N, "dx")
        w1_words, w2_words = words(M, "w1_words"), words(M, "w2_words")
        x_words = words(N, "x_words")
        dx_words = [words(HALF, "dx_words%d" % h) for h in range(2)]

        interleave(nc.scalar.copy, x_words, x_raw, slice(0, SCALAR_COLS_X))
        interleave(nc.vector.tensor_copy, x_words, x_raw, halves[1])
        interleave(nc.vector.tensor_copy, x_words, x_raw, slice(SCALAR_COLS_X, HALF))
        interleave(nc.scalar.copy, w1_words, w1_raw, all_m)
        for cols in reversed(halves):
            quantize(x_q, x_words, cols)
        quantize(w1_q, w1_words, all_m)

        bank_a = [ps.tile([P, N], F32, name="bank_a%d" % g) for g in range(G)]
        bank_b = [ps.tile([P, N], F32, name="bank_b%d" % g) for g in range(G)]
        for g in range(G - 1):
            product(bank_a[g], w1_q, x_q, g)

        sum_sq, inv_ms, gain_inv = columns("sum_sq"), columns("inv_ms"), columns("gain_inv")
        neg_c, sum_p = columns("neg_c"), columns("sum_p")
        neg_mean_q, neg_mean = columns("neg_mean_q"), columns("neg_mean")
        z1n, u, p_term, q_term = rows_of("z1n"), rows_of("u"), rows_of("p_term"), rows_of("q_term")
        result = rows_of("result")

        def make_gain_inv(g):
            nc.scalar.activation(out=gain_inv[g][:], in_=inv_ms[g][:], func=ACT.Copy, scale=gain[g])

        def normalise(g):
            nc.scalar.activation(out=z1n[g][:], in_=bank_a[g][:], func=ACT.Square, accum_out=sum_sq[g][:])
            if g > 0:
                make_gain_inv(g - 1)
            nc.scalar.activation(
                out=inv_ms[g][:], in_=sum_sq[g][:], func=ACT.Abs_reciprocal_sqrt, scale=1.0 / N, bias=eps[:]
            )
            nc.scalar.activation(out=z1n[g][:], in_=bank_a[g][:], func=ACT.Copy, scale=inv_ms[g][:])
            if g == G - 1:
                make_gain_inv(g)

        def make_q(g):
            nc.vector.scalar_tensor_tensor(
                out=q_term[g][:], in0=bank_a[g][:], scalar=gain[g], in1=z1n[g][:],
                op0=ALU.mult, op1=ALU.mult,
            )
            product(bank_a[g], w2_q, x_q, g)
            nc.gpsimd.tensor_tensor(out=base_sb[g][:], in0=q_term[g][:], in1=base_sb[g][:], op=ALU.add)

        def make_c(g):
            nc.vector.scalar_tensor_tensor(
                out=u[g][:], in0=bank_b[g][:], scalar=-1.0 / N, in1=z1n[g][:],
                op0=ALU.mult, op1=ALU.mult, accum_out=neg_c[g][:],
            )

        def make_u(g):
            nc.vector.scalar_tensor_tensor(
                out=u[g][:], in0=z1n[g][:], scalar=neg_c[g][:], in1=bank_b[g][:], op0=ALU.mult, op1=ALU.add
            )

        def make_p(g):
            nc.vector.scalar_tensor_tensor(
                out=p_term[g][:], in0=bank_a[g][:], scalar=gain_inv[g][:], in1=u[g][:],
                op0=ALU.mult, op1=ALU.mult, accum_out=sum_p[g][:],
            )

        def mean_of_q(g):
            nc.scalar.activation(
                out=result[g][:], in_=q_term[g][:], func=ACT.Copy, scale=-1.0 / N, accum_out=neg_mean_q[g][:]
            )

        def make_mean(g):
            nc.scalar.activation(
                out=neg_mean[g][:], in_=sum_p[g][:], func=ACT.Identity, scale=-1.0 / N, bias=neg_mean_q[g][:]
            )

        def add_p(g):
            nc.gpsimd.tensor_tensor(out=base_sb[g][:], in0=p_term[g][:], in1=base_sb[g][:], op=ALU.add)

        def centre_and_store(g):
            nc.scalar.activation(out=result[g][:], in_=base_sb[g][:], func=ACT.Identity, bias=neg_mean[g][:])
            nc.scalar.dma_start(out=out[g], in_=result[g][:])

        def finish_on_vector(g, cols):
            nc.vector.scalar_tensor_tensor(
                out=result[g][:, cols], in0=p_term[g][:, cols], scalar=neg_mean[g][:], in1=base_sb[g][:, cols],
                op0=ALU.add, op1=ALU.add,
            )
            nc.sync.dma_start(out=out[g][:, cols], in_=result[g][:, cols])

        def tangents(g):
            product(bank_b[g], w1_q, dx_q, g)
            product(bank_a[g], w2_q, dx_q, g)

        interleave(nc.scalar.copy, dx_words[0], dx_raw[0], quarters[0])
        interleave(nc.vector.tensor_copy, dx_words[0], dx_raw[0], quarters[1])
        quantize(dx_q, dx_words[0], slice(0, HALF))
        for cols in quarters:
            interleave(nc.vector.tensor_copy, dx_words[1], dx_raw[1], cols)
        for cols in quarters:
            quantize(dx_q, dx_words[1], cols, HALF)
        interleave(nc.vector.tensor_copy, w2_words, w2_raw, all_m)
        nc.vector.transpose(out=og_cols[:], in_=og_rows[:])
        quantize(w2_q, w2_words, all_m)

        normalise(0)
        tangents(0)
        product(bank_a[G - 1], w1_q, x_q, G - 1)
        normalise(1)
        tangents(1)
        for g in range(G):
            make_c(g)
            make_q(g)
            if g + 2 < G:
                normalise(g + 2)
                tangents(g + 2)
            mean_of_q(g)
            if g >= 2:
                centre_and_store(g - 2)
            make_u(g)
            if g > 0:
                make_p(g - 1)
                make_mean(g - 1)
                if g - 1 < G - 2:
                    add_p(g - 1)
        make_p(G - 1)
        make_mean(G - 1)
        for g in range(G - 2, G):
            for cols in halves:
                finish_on_vector(g, cols)
